import numpy as np
import ml_dtypes


def mxq(x, axis, fmt="e4m3"):
    dtype, down = {"e4m3": (ml_dtypes.float8_e4m3fn, 7), "e5m2": (ml_dtypes.float8_e5m2, 14)}[fmt]
    v = np.moveaxis(np.asarray(x, np.float32).astype(ml_dtypes.bfloat16).astype(np.float64), axis, -1)
    blocks = v.reshape(v.shape[:-1] + (-1, 32))
    amax = np.abs(blocks).max(-1, keepdims=True)
    byte = np.maximum(np.where(amax > 0, np.frexp(amax)[1] - 1 + 127, 0) - down, 1)
    scale = np.exp2(byte - 127.0)
    codes = (blocks / scale).astype(np.float32).astype(dtype).astype(np.float64)
    return np.moveaxis((codes * scale).reshape(v.shape), -1, axis)


WIDE = False


def mx_kscale(k):
    if not WIDE:
        return np.ones(k)
    levels = np.array([10, -10, 5, -5, 0])
    if k % 512:
        return np.exp2(np.random.permutation(np.resize(levels, k // 32))).repeat(32)
    a = np.empty((k // 512, 16))
    for p in range(k // 512):
        a[p, :8] = np.random.permutation(np.resize(levels, 8))
        for g in range(8):
            far = levels[np.abs(levels - a[p, g]) >= 10]
            a[p, g + 8] = far[np.random.randint(len(far))]
    return np.exp2(a.ravel()).repeat(32)


def f64(x):
    return np.asarray(x).astype(np.float64)


def striped(idx):
    return np.tile(np.asarray(idx).reshape(-1, 16).T, (8, 1)).astype(np.uint16)


def unstriped(offs):
    return offs[:16].T.reshape(-1).astype(np.int64)


E2M1 = np.array([0.0, 0.5, 1.0, 1.5, 2.0, 3.0, 4.0, 6.0, -0.0, -0.5, -1.0, -1.5, -2.0, -3.0, -4.0, -6.0])


def pack_weight(w, fmt):
    k, n = w.shape
    w = f64(np.asarray(w, np.float32).astype(ml_dtypes.bfloat16)).reshape(k // 32, 32, n)
    amax = np.abs(w).max(1)
    if fmt == "e4m3":
        byte = np.frexp(amax)[1] - 1 + 127 - 7
    else:
        mant, ex = np.frexp(amax / 6.0)
        byte = np.where(mant > 0.5, ex, ex - 1) + 127
    byte = np.clip(np.where(amax > 0, byte, 1), 1, 254)
    scaled = (w * np.exp2(127.0 - byte)[:, None, :]).reshape(k, n).astype(np.float32)
    by_word = np.ascontiguousarray(scaled.reshape(k // 512, 128, 4, n).transpose(0, 1, 3, 2))
    if fmt == "e4m3":
        words = by_word.astype(ml_dtypes.float8_e4m3fn).view(np.uint8)
    else:
        c = by_word.astype(ml_dtypes.float4_e2m1fn).view(np.uint8) & 0xF
        words = (c[..., 0::2] | (c[..., 1::2] << 4)).reshape(k // 512, 128, 2 * n)
    return np.ascontiguousarray(words), np.ascontiguousarray(byte.astype(np.uint8).reshape(k // 512, 16, n))


def unpack_weight(words, scales, fmt):
    g, _, n = scales.shape
    words = np.ascontiguousarray(words).reshape(g, 128, n, -1)
    if fmt == "e4m3":
        vals = words.view(ml_dtypes.float8_e4m3fn).astype(np.float64)
    else:
        nib = np.empty((g, 128, n, 4), np.uint8)
        nib[..., 0::2] = words & 0xF
        nib[..., 1::2] = words >> 4
        vals = E2M1[nib]
    vals = vals * np.repeat(np.exp2(scales.astype(np.float64) - 127.0), 8, axis=1)[..., None]
    return vals.transpose(0, 1, 3, 2).reshape(g * 512, n)


D, T, I, Q, E, U = 512, 2048, 512, 128, 512, 512


def setup_inputs():
    n = np.random.standard_normal
    idx = np.random.permutation(T)[:I]
    idx2 = np.random.randint(0, U, I)
    fd = mx_kscale(D)
    fi = mx_kscale(I)
    ti = np.ones(T)
    ti[idx] = fi
    keysp = pack_weight(n((D, T)) / fd[:, None], "e4m3")
    return {
        "query": (n((D, Q)) * 0.25 / np.sqrt(D) * fd[:, None]).astype(np.float32),
        "keys_words": keysp[0],
        "keys_scales": keysp[1],
        "pquery": (n((D, Q)) * 1.0 / np.sqrt(D) * fd[:, None]).astype(np.float32),
        "pgsum": (n((D, U)) / fd[:, None]).astype(np.float32),
        "th": (np.random.uniform(-0.8, 0.2, (Q, 1))).astype(np.float32),
        "size": (np.random.uniform(0.5, 2.0, (1, I)) * fi).astype(np.float32),
        "vals": (n((E, T)) / ti).astype(np.float32),
        "offs": striped(idx),
        "offs2": striped(idx2),
    }


def reference(query, keys_words, keys_scales, pquery, pgsum, th, size, vals, offs, offs2):
    idx = unstriped(offs)
    idx2 = unstriped(offs2)
    keysu = unpack_weight(keys_words, keys_scales, "e4m3")
    pqueryq = mxq(f64(pquery), 0, "e4m3")
    pgsumq = mxq(f64(pgsum), 0, "e4m3")
    b = pqueryq.T @ pgsumq
    ex = np.maximum(b - f64(th), 0.05)
    queryq = mxq(f64(query), 0, "e4m3")
    keysidxg = keysu[:, idx]
    a = queryq.T @ keysidxg
    p = np.exp(a - np.max(a, axis=1, keepdims=True)) * ex[:, idx2]
    w = p * f64(size) / np.sum(p, axis=1, keepdims=True)
    wt = w.T
    vt = f64(vals)[:, idx].T
    wtq = mxq(wt, 0, "e4m3")
    vtq = mxq(vt, 0, "e4m3")
    o = wtq.T @ vtq
    return o

@@ -1,0 +1,205 @@
+from contextlib import ExitStack
+
+import concourse.mybir as mybir
+from concourse.masks import make_identity
+
+D, T, I, Q, E, U = 512, 2048, 512, 128, 512, 512
+FLOPS = 2 * D * Q * U + 2 * D * Q * I + 2 * I * Q * E
+
+F32 = mybir.dt.float32
+BF16 = mybir.dt.bfloat16
+I32 = mybir.dt.int32
+U32 = mybir.dt.uint32
+U16 = mybir.dt.uint16
+U8 = mybir.dt.uint8
+FP8X4 = mybir.dt.float8_e4m3fn_x4
+ALU = mybir.AluOpType
+ACT = mybir.ActivationFunctionType
+
+P = 128
+PACK = 4
+FLOOR = 0.05
+BLOCKS = E // P
+
+
+def interleave(copy, grouped, raw):
+    copy(
+        out=grouped.rearrange("p (c i) t -> p c t i", i=4),
+        in_=raw.rearrange("p t (c i) -> p c t i", i=4),
+    )
+
+
+def quantize(nc, codes, scales, grouped):
+    nc.vector.quantize_mx(out=codes.bitcast(FP8X4), scales=scales, in_=grouped.rearrange("p c t -> p (c t)"))
+
+
+def product(nc, acc, lhs_codes, lhs_scales, rhs_codes, rhs_scales):
+    nc.tensor.matmul_mx(
+        out=acc,
+        lhsT=lhs_codes.bitcast(FP8X4),
+        lhsT_scale=lhs_scales,
+        rhs=rhs_codes.bitcast(FP8X4),
+        rhs_scale=rhs_scales,
+        start=True,
+        stop=True,
+    )
+
+
+def turn(nc, turned, grouped, rows, ident):
+    words = rows.bitcast(F32)
+    for u in range(2):
+        nc.tensor.transpose(turned[:, u, :], words[:, u::2], ident)
+    nc.scalar.copy(
+        out=grouped.rearrange("p c t -> p (c t)").bitcast(F32).rearrange("p (c u) -> p c u", u=2),
+        in_=turned.rearrange("p u c -> p c u"),
+    )
+
+
+def tile_attend_pagethreshold_kernel(
+    tc, query, keys_words, keys_scales, pquery, pgsum, th, size, vals, offs, offs2, out
+):
+    nc = tc.nc
+    with ExitStack() as ctx:
+        lists = ctx.enter_context(tc.tile_pool(name="lists", bufs=1))
+        sb = ctx.enter_context(tc.tile_pool(name="sb", bufs=1))
+        ps = ctx.enter_context(tc.psum_pool(name="ps", bufs=1))
+        ring = ctx.enter_context(tc.psum_pool(name="ring", bufs=2))
+
+        token_list = lists.tile([P, I // 16], U16)
+        page_list = lists.tile([P, I // 16], U16)
+        pq_raw = sb.tile([P, PACK, Q], F32)
+        pg_raw = sb.tile([P, PACK, U], F32)
+        q_raw = sb.tile([P, PACK, Q], F32)
+        warm = sb.tile([P, 1], F32)
+        key_words = sb.tile([P, T], U32)
+        key_bytes = sb.tile([P, T], U8, tag="after0", align_bytes=64)
+        th_col = sb.tile([P, 1], F32, align_bytes=64, tag="after_excess")
+        size_cols = sb.tile([P, PACK], F32)
+
+        nc.vector.memset(key_bytes[:].bitcast(I32), 0)
+        nc.scalar.dma_start(out=th_col[:], in_=th)
+        nc.gpsimd.memset(warm[:], 0.0)
+        nc.scalar.activation(out=warm[:], in_=warm[:], func=ACT.Exp)
+        nc.sync.dma_start(out=pq_raw[:], in_=pquery.rearrange("(p t) c -> p t c", t=PACK))
+        nc.sync.dma_start(out=pg_raw[:], in_=pgsum.rearrange("(p t) c -> p t c", t=PACK))
+        nc.sync.dma_start(token_list[:], offs)
+        byte_rows = keys_scales[0].bitcast(I32).rearrange("(g r) n -> r g n", r=4)
+        for r in range(4):
+            nc.sync.dma_start(out=key_bytes[r:P:32, :].bitcast(I32), in_=byte_rows[r])
+        nc.sync.dma_start(out=q_raw[:], in_=query.rearrange("(p t) c -> p t c", t=PACK))
+        nc.sync.dma_start(
+            out=key_words[:].bitcast(I32), in_=keys_words[0].rearrange("p n t -> p (n t)").bitcast(I32)
+        )
+        nc.sync.dma_start(page_list[:], offs2)
+        nc.sync.dma_start(out=size_cols[:], in_=size.rearrange("o (p t) -> (o p) t", t=PACK))
+        val_pool = [sb.tile([P, T], F32, name="val_pool%d" % c, tag="pool%d" % c, align_bytes=64) for c in range(BLOCKS)]
+        for c in range(BLOCKS):
+            nc.sync.dma_start(out=val_pool[c][:], in_=vals[c * P : (c + 1) * P, :])
+
+        ident = sb.tile([P, P], F32)
+        make_identity(nc, ident[:])
+
+
+        pq_grouped = sb.tile([P, Q, PACK], BF16, align_bytes=64)
+        pq_codes = sb.tile([P, Q], U32, align_bytes=64)
+        pq_scales = sb.tile([P, Q], U8, align_bytes=64)
+        interleave(nc.scalar.copy, pq_grouped[:], pq_raw[:])
+        quantize(nc, pq_codes[:], pq_scales[:], pq_grouped[:])
+
+        pg_codes = sb.tile([P, U], U32, align_bytes=64)
+        pg_scales = sb.tile([P, U], U8, align_bytes=64)
+        for h, copy in enumerate((nc.vector.tensor_copy, nc.scalar.copy)):
+            cols = slice(h * U // 2, (h + 1) * U // 2)
+            pg_grouped = sb.tile([P, U // 2, PACK], BF16, align_bytes=64, name="pg_grouped%d" % h)
+            interleave(copy, pg_grouped[:], pg_raw[:, :, cols])
+            quantize(nc, pg_codes[:, cols], pg_scales[:, cols], pg_grouped[:])
+        page_scores = ps.tile([P, U], F32)
+        product(nc, page_scores[:], pq_codes[:], pq_scales[:], pg_codes[:], pg_scales[:])
+
+        k_scales = sb.tile([P, I], U8, align_bytes=64)
+        nc.vector.tensor_copy(out=k_scales[:], in_=key_bytes[:].indirect(token_list[:]))
+
+        q_grouped = sb.tile([P, Q, PACK], BF16, align_bytes=64)
+        q_codes = sb.tile([P, Q], U32, align_bytes=64)
+        q_scales = sb.tile([P, Q], U8, align_bytes=64)
+        interleave(nc.scalar.copy, q_grouped[:], q_raw[:])
+        quantize(nc, q_codes[:], q_scales[:], q_grouped[:])
+
+        excess = sb.tile([P, U], F32, tag="after0", align_bytes=64)
+        nc.vector.tensor_scalar(excess[:], page_scores[:], th_col[:], FLOOR, ALU.subtract, ALU.max)
+
+        k_codes = sb.tile([P, I], U32, align_bytes=64, tag="after_excess")
+        nc.vector.tensor_copy(out=k_codes[:], in_=key_words[:].indirect(token_list[:]))
+        scores = ps.tile([P, I], F32)
+        product(nc, scores[:], q_codes[:], q_scales[:], k_codes[:], k_scales[:])
+
+        gate = sb.tile([P, I], F32)
+        for h in range(2):
+            nc.vector.tensor_copy(
+                out=gate[:, h * I // 2 : (h + 1) * I // 2],
+                in_=excess[:].indirect(page_list[:, h * I // 32 : (h + 1) * I // 32]),
+            )
+
+        size_rows = ps.tile([P, PACK, P], F32)
+        for t in range(PACK):
+            nc.tensor.transpose(size_rows[:, t, :], size_cols[:, t : t + 1].to_broadcast([P, P]), ident[:])
+
+        neg_max = sb.tile([P, 1], F32)
+        nc.vector.tensor_reduce(neg_max[:], scores[:], mybir.AxisListType.X, ALU.max, negate=True)
+        expd = sb.tile([P, I], F32)
+        nc.scalar.activation(out=expd[:], in_=scores[:], func=ACT.Exp, bias=neg_max[:], scale=1.0)
+
+        v_codes = [sb.tile([P, P], U32, align_bytes=64, name="v_codes%d" % c, tag=("v_codes0", "pool2", "pool3", "v_codes3")[c]) for c in range(BLOCKS)]
+        v_scales = [sb.tile([P, P], U8, align_bytes=64, name="v_scales%d" % c) for c in range(BLOCKS)]
+        v_grouped = [sb.tile([P, P, PACK], BF16, align_bytes=64, name="v_grouped%d" % c) for c in range(BLOCKS)]
+
+        def gather_values(c):
+            listed = sb.tile([P, I], BF16, name="listed%d" % c, tag=("after0", "pool0", "listed2", "listed3")[c], align_bytes=64)
+            nc.vector.tensor_copy(out=listed[:], in_=val_pool[c][:].indirect(token_list[:]))
+            turned = ring.tile([P, 2, P], F32, name="turned")
+            turn(nc, turned[:], v_grouped[c][:], listed[:], ident[:])
+
+        gather_values(0)
+
+        weights = sb.tile([P, I], F32, tag="pool0", align_bytes=64)
+        row_sum = sb.tile([P, 1], F32)
+        nc.vector.scalar_tensor_tensor(weights[:], expd[:], 1.0, gate[:], ALU.mult, ALU.mult, accum_out=row_sum[:])
+        quantize(nc, v_codes[0][:], v_scales[0][:], v_grouped[0][:])
+        inv_sum = sb.tile([P, 1], F32)
+        nc.vector.reciprocal(inv_sum[:], row_sum[:])
+        w_rows = sb.tile([P, I], BF16)
+        nc.vector.scalar_tensor_tensor(
+            w_rows[:].rearrange("p (s t) -> p s t", t=PACK),
+            weights[:].rearrange("p (s t) -> p s t", t=PACK),
+            inv_sum[:],
+            size_rows[:].rearrange("p t s -> p s t"),
+            ALU.mult,
+            ALU.mult,
+        )
+        w_turned = ps.tile([P, 2, P], F32)
+        w_grouped = sb.tile([P, Q, PACK], BF16, align_bytes=64)
+        turn(nc, w_turned[:], w_grouped[:], w_rows[:], ident[:])
+
+        gather_values(1)
+        w_codes = sb.tile([P, Q], U32, align_bytes=64, tag="pool1")
+        w_scales = sb.tile([P, Q], U8, align_bytes=64)
+        quantize(nc, w_codes[:], w_scales[:], w_grouped[:])
+
+        early = sb.tile([P, (BLOCKS - 1) * P], F32)
+        last = sb.tile([P, P], F32)
+
+        def multiply(c, result):
+            acc = ring.tile([P, P], F32, name="acc")
+            product(nc, acc[:], w_codes[:], w_scales[:], v_codes[c][:], v_scales[c][:])
+            nc.scalar.copy(out=result, in_=acc[:])
+
+        multiply(0, early[:, 0:P])
+        for c in range(1, BLOCKS):
+            if c + 1 < BLOCKS:
+                gather_values(c + 1)
+            quantize(nc, v_codes[c][:], v_scales[c][:], v_grouped[c][:])
+            if c < BLOCKS - 1:
+                multiply(c, early[:, c * P : (c + 1) * P])
+        nc.sync.dma_start(out=out[:, 0 : (BLOCKS - 1) * P], in_=early[:])
+        multiply(BLOCKS - 1, last[:])
+        nc.sync.dma_start(out=out[:, (BLOCKS - 1) * P : E], in_=last[:])

@@ -65,16 +65,20 @@ def tile_attend_pagethreshold_kernel(
         ps = ctx.enter_context(tc.psum_pool(name="ps", bufs=1))
         ring = ctx.enter_context(tc.psum_pool(name="ring", bufs=2))
 
+        def tile(shape, dtype, name, takes_over=None):
+            return sb.tile(shape, dtype, name=name, tag=takes_over or name, align_bytes=64)
+
         token_list = lists.tile([P, I // 16], U16)
         page_list = lists.tile([P, I // 16], U16)
-        pq_raw = sb.tile([P, PACK, Q], F32)
-        pg_raw = sb.tile([P, PACK, U], F32)
-        q_raw = sb.tile([P, PACK, Q], F32)
-        warm = sb.tile([P, 1], F32)
-        key_words = sb.tile([P, T], U32)
-        key_bytes = sb.tile([P, T], U8, tag="after0", align_bytes=64)
-        th_col = sb.tile([P, 1], F32, align_bytes=64, tag="after_excess")
-        size_cols = sb.tile([P, PACK], F32)
+        pq_raw = tile([P, PACK, Q], F32, "pq_raw")
+        pg_raw = tile([P, PACK, U], F32, "pg_raw")
+        q_raw = tile([P, PACK, Q], F32, "q_raw")
+        warm = tile([P, 1], F32, "warm")
+        key_words = tile([P, T], U32, "key_words")
+        key_bytes = tile([P, T], U8, "key_bytes")
+        th_col = tile([P, 1], F32, "th_col")
+        size_cols = tile([P, PACK], F32, "size_cols")
+        val_pool = [tile([P, T], F32, "val_pool%d" % c) for c in range(BLOCKS)]
 
         nc.vector.memset(key_bytes[:].bitcast(I32), 0)
         nc.scalar.dma_start(out=th_col[:], in_=th)
@@ -92,48 +96,51 @@ def tile_attend_pagethreshold_kernel(
         )
         nc.sync.dma_start(page_list[:], offs2)
         nc.sync.dma_start(out=size_cols[:], in_=size.rearrange("o (p t) -> (o p) t", t=PACK))
-        val_pool = [sb.tile([P, T], F32, name="val_pool%d" % c, tag="pool%d" % c, align_bytes=64) for c in range(BLOCKS)]
         for c in range(BLOCKS):
             nc.sync.dma_start(out=val_pool[c][:], in_=vals[c * P : (c + 1) * P, :])
 
-        ident = sb.tile([P, P], F32)
+        ident = tile([P, P], F32, "ident")
         make_identity(nc, ident[:])
 
-
-        pq_grouped = sb.tile([P, Q, PACK], BF16, align_bytes=64)
-        pq_codes = sb.tile([P, Q], U32, align_bytes=64)
-        pq_scales = sb.tile([P, Q], U8, align_bytes=64)
+        pq_grouped = tile([P, Q, PACK], BF16, "pq_grouped")
+        pq_codes = tile([P, Q], U32, "pq_codes")
+        pq_scales = tile([P, Q], U8, "pq_scales")
         interleave(nc.scalar.copy, pq_grouped[:], pq_raw[:])
         quantize(nc, pq_codes[:], pq_scales[:], pq_grouped[:])
 
-        pg_codes = sb.tile([P, U], U32, align_bytes=64)
-        pg_scales = sb.tile([P, U], U8, align_bytes=64)
+        pg_codes = tile([P, U], U32, "pg_codes")
+        pg_scales = tile([P, U], U8, "pg_scales")
         for h, copy in enumerate((nc.vector.tensor_copy, nc.scalar.copy)):
             cols = slice(h * U // 2, (h + 1) * U // 2)
-            pg_grouped = sb.tile([P, U // 2, PACK], BF16, align_bytes=64, name="pg_grouped%d" % h)
+            pg_grouped = tile([P, U // 2, PACK], BF16, "pg_grouped%d" % h)
             interleave(copy, pg_grouped[:], pg_raw[:, :, cols])
             quantize(nc, pg_codes[:, cols], pg_scales[:, cols], pg_grouped[:])
         page_scores = ps.tile([P, U], F32)
         product(nc, page_scores[:], pq_codes[:], pq_scales[:], pg_codes[:], pg_scales[:])
 
-        k_scales = sb.tile([P, I], U8, align_bytes=64)
+        k_scales = tile([P, I], U8, "k_scales")
         nc.vector.tensor_copy(out=k_scales[:], in_=key_bytes[:].indirect(token_list[:]))
 
-        q_grouped = sb.tile([P, Q, PACK], BF16, align_bytes=64)
-        q_codes = sb.tile([P, Q], U32, align_bytes=64)
-        q_scales = sb.tile([P, Q], U8, align_bytes=64)
+        q_grouped = tile([P, Q, PACK], BF16, "q_grouped")
+        q_codes = tile([P, Q], U32, "q_codes")
+        q_scales = tile([P, Q], U8, "q_scales")
         interleave(nc.scalar.copy, q_grouped[:], q_raw[:])
         quantize(nc, q_codes[:], q_scales[:], q_grouped[:])
 
-        excess = sb.tile([P, U], F32, tag="after0", align_bytes=64)
-        nc.vector.tensor_scalar(excess[:], page_scores[:], th_col[:], FLOOR, ALU.subtract, ALU.max)
+        shift = tile([P, 1], F32, "shift")
+        nc.gpsimd.tensor_scalar(shift[:], th_col[:], -1.0, -FLOOR, ALU.mult, ALU.add)
+        above = tile([P, U], F32, "above", takes_over="q_raw")
+        nc.scalar.activation(out=above[:], in_=page_scores[:], func=ACT.Relu, bias=shift[:], scale=1.0)
+        excess = tile([P, U], F32, "excess")
+        nc.scalar.activation(out=excess[:], in_=above[:], func=ACT.Copy, bias=FLOOR, scale=1.0)
 
-        k_codes = sb.tile([P, I], U32, align_bytes=64, tag="after_excess")
+        k_codes = tile([P, I], U32, "k_codes")
         nc.vector.tensor_copy(out=k_codes[:], in_=key_words[:].indirect(token_list[:]))
+
         scores = ps.tile([P, I], F32)
         product(nc, scores[:], q_codes[:], q_scales[:], k_codes[:], k_scales[:])
 
-        gate = sb.tile([P, I], F32)
+        gate = tile([P, I], F32, "gate")
         for h in range(2):
             nc.vector.tensor_copy(
                 out=gate[:, h * I // 2 : (h + 1) * I // 2],
@@ -144,30 +151,29 @@ def tile_attend_pagethreshold_kernel(
         for t in range(PACK):
             nc.tensor.transpose(size_rows[:, t, :], size_cols[:, t : t + 1].to_broadcast([P, P]), ident[:])
 
-        neg_max = sb.tile([P, 1], F32)
+        neg_max = tile([P, 1], F32, "neg_max")
         nc.vector.tensor_reduce(neg_max[:], scores[:], mybir.AxisListType.X, ALU.max, negate=True)
-        expd = sb.tile([P, I], F32)
+        expd = tile([P, I], F32, "expd")
         nc.scalar.activation(out=expd[:], in_=scores[:], func=ACT.Exp, bias=neg_max[:], scale=1.0)
 
-        v_codes = [sb.tile([P, P], U32, align_bytes=64, name="v_codes%d" % c, tag=("v_codes0", "pool2", "pool3", "v_codes3")[c]) for c in range(BLOCKS)]
-        v_scales = [sb.tile([P, P], U8, align_bytes=64, name="v_scales%d" % c) for c in range(BLOCKS)]
-        v_grouped = [sb.tile([P, P, PACK], BF16, align_bytes=64, name="v_grouped%d" % c) for c in range(BLOCKS)]
+        grouped = tile([P, BLOCKS * P, PACK], BF16, "grouped")
+        last_grouped = tile([P, P, PACK], BF16, "last_grouped")
 
         def gather_values(c):
-            listed = sb.tile([P, I], BF16, name="listed%d" % c, tag=("after0", "pool0", "listed2", "listed3")[c], align_bytes=64)
+            listed = tile([P, I], BF16, "listed%d" % c)
             nc.vector.tensor_copy(out=listed[:], in_=val_pool[c][:].indirect(token_list[:]))
             turned = ring.tile([P, 2, P], F32, name="turned")
-            turn(nc, turned[:], v_grouped[c][:], listed[:], ident[:])
+            target = last_grouped[:] if c == BLOCKS - 1 else grouped[:, (c + 1) * P : (c + 2) * P, :]
+            turn(nc, turned[:], target, listed[:], ident[:])
 
         gather_values(0)
 
-        weights = sb.tile([P, I], F32, tag="pool0", align_bytes=64)
-        row_sum = sb.tile([P, 1], F32)
+        weights = tile([P, I], F32, "weights", takes_over="val_pool0")
+        row_sum = tile([P, 1], F32, "row_sum")
         nc.vector.scalar_tensor_tensor(weights[:], expd[:], 1.0, gate[:], ALU.mult, ALU.mult, accum_out=row_sum[:])
-        quantize(nc, v_codes[0][:], v_scales[0][:], v_grouped[0][:])
-        inv_sum = sb.tile([P, 1], F32)
+        inv_sum = tile([P, 1], F32, "inv_sum")
         nc.vector.reciprocal(inv_sum[:], row_sum[:])
-        w_rows = sb.tile([P, I], BF16)
+        w_rows = tile([P, I], BF16, "w_rows")
         nc.vector.scalar_tensor_tensor(
             w_rows[:].rearrange("p (s t) -> p s t", t=PACK),
             weights[:].rearrange("p (s t) -> p s t", t=PACK),
@@ -177,29 +183,26 @@ def tile_attend_pagethreshold_kernel(
             ALU.mult,
         )
         w_turned = ps.tile([P, 2, P], F32)
-        w_grouped = sb.tile([P, Q, PACK], BF16, align_bytes=64)
-        turn(nc, w_turned[:], w_grouped[:], w_rows[:], ident[:])
+        turn(nc, w_turned[:], grouped[:, :P, :], w_rows[:], ident[:])
 
-        gather_values(1)
-        w_codes = sb.tile([P, Q], U32, align_bytes=64, tag="pool1")
-        w_scales = sb.tile([P, Q], U8, align_bytes=64)
-        quantize(nc, w_codes[:], w_scales[:], w_grouped[:])
-
-        early = sb.tile([P, (BLOCKS - 1) * P], F32)
-        last = sb.tile([P, P], F32)
-
-        def multiply(c, result):
-            acc = ring.tile([P, P], F32, name="acc")
-            product(nc, acc[:], w_codes[:], w_scales[:], v_codes[c][:], v_scales[c][:])
-            nc.scalar.copy(out=result, in_=acc[:])
-
-        multiply(0, early[:, 0:P])
         for c in range(1, BLOCKS):
-            if c + 1 < BLOCKS:
-                gather_values(c + 1)
-            quantize(nc, v_codes[c][:], v_scales[c][:], v_grouped[c][:])
-            if c < BLOCKS - 1:
-                multiply(c, early[:, c * P : (c + 1) * P])
+            gather_values(c)
+
+        codes = tile([P, BLOCKS * P], U32, "codes", takes_over="val_pool3")
+        scales = tile([P, BLOCKS * P], U8, "scales")
+        quantize(nc, codes[:], scales[:], grouped[:])
+        early = tile([P, (BLOCKS - 1) * P], F32, "early")
+        for lo, hi in ((0, 2 * P), (2 * P, 3 * P)):
+            acc = ring.tile([P, hi - lo], F32, name="acc")
+            product(nc, acc[:], codes[:, :P], scales[:, :P], codes[:, P + lo : P + hi], scales[:, P + lo : P + hi])
+            nc.scalar.copy(out=early[:, lo:hi], in_=acc[:])
         nc.sync.dma_start(out=out[:, 0 : (BLOCKS - 1) * P], in_=early[:])
-        multiply(BLOCKS - 1, last[:])
+
+        last_codes = tile([P, P], U32, "last_codes")
+        last_scales = tile([P, P], U8, "last_scales")
+        quantize(nc, last_codes[:], last_scales[:], last_grouped[:])
+        last_acc = ps.tile([P, P], F32, name="last_acc", tag="page_scores")
+        product(nc, last_acc[:], codes[:, :P], scales[:, :P], last_codes[:], last_scales[:])
+        last = tile([P, P], F32, "last")
+        nc.vector.tensor_copy(out=last[:], in_=last_acc[:])
         nc.sync.dma_start(out=out[:, (BLOCKS - 1) * P : E], in_=last[:])

@@ -95,8 +95,9 @@ def tile_attend_pagethreshold_kernel(
             out=key_words[:].bitcast(I32), in_=keys_words[0].rearrange("p n t -> p (n t)").bitcast(I32)
         )
         nc.sync.dma_start(page_list[:], offs2)
-        nc.sync.dma_start(out=size_cols[:], in_=size.rearrange("o (p t) -> (o p) t", t=PACK))
         for c in range(BLOCKS):
+            if c == BLOCKS - 1:
+                nc.sync.dma_start(out=size_cols[:], in_=size.rearrange("o (p t) -> (o p) t", t=PACK))
             nc.sync.dma_start(out=val_pool[c][:], in_=vals[c * P : (c + 1) * P, :])
 
         ident = tile([P, P], F32, "ident")
@@ -147,10 +148,6 @@ def tile_attend_pagethreshold_kernel(
                 in_=excess[:].indirect(page_list[:, h * I // 32 : (h + 1) * I // 32]),
             )
 
-        size_rows = ps.tile([P, PACK, P], F32)
-        for t in range(PACK):
-            nc.tensor.transpose(size_rows[:, t, :], size_cols[:, t : t + 1].to_broadcast([P, P]), ident[:])
-
         neg_max = tile([P, 1], F32, "neg_max")
         nc.vector.tensor_reduce(neg_max[:], scores[:], mybir.AxisListType.X, ALU.max, negate=True)
         expd = tile([P, I], F32, "expd")
@@ -173,36 +170,42 @@ def tile_attend_pagethreshold_kernel(
         nc.vector.scalar_tensor_tensor(weights[:], expd[:], 1.0, gate[:], ALU.mult, ALU.mult, accum_out=row_sum[:])
         inv_sum = tile([P, 1], F32, "inv_sum")
         nc.vector.reciprocal(inv_sum[:], row_sum[:])
-        w_rows = tile([P, I], BF16, "w_rows")
-        nc.vector.scalar_tensor_tensor(
-            w_rows[:].rearrange("p (s t) -> p s t", t=PACK),
-            weights[:].rearrange("p (s t) -> p s t", t=PACK),
-            inv_sum[:],
-            size_rows[:].rearrange("p t s -> p s t"),
-            ALU.mult,
+        normed = tile([P, PACK, P], F32, "normed")
+        nc.scalar.activation(
+            out=normed[:].rearrange("q t s -> q s t"),
+            in_=weights[:].rearrange("q (s t) -> q s t", t=PACK),
+            func=ACT.Copy,
+            scale=inv_sum[:],
+        )
+        w_turned = ps.tile([P, PACK, Q], F32)
+        for t in range(PACK):
+            nc.tensor.transpose(w_turned[:, t, :], normed[:, t, :], ident[:])
+
+        gather_values(1)
+        gather_values(2)
+        nc.vector.tensor_tensor(
+            grouped[:, :P, :],
+            w_turned[:].rearrange("p t q -> p q t"),
+            size_cols[:].unsqueeze(1).to_broadcast([P, Q, PACK]),
             ALU.mult,
         )
-        w_turned = ps.tile([P, 2, P], F32)
-        turn(nc, w_turned[:], grouped[:, :P, :], w_rows[:], ident[:])
-
-        for c in range(1, BLOCKS):
-            gather_values(c)
+        gather_values(3)
 
         codes = tile([P, BLOCKS * P], U32, "codes", takes_over="val_pool3")
         scales = tile([P, BLOCKS * P], U8, "scales")
         quantize(nc, codes[:], scales[:], grouped[:])
-        early = tile([P, (BLOCKS - 1) * P], F32, "early")
-        for lo, hi in ((0, 2 * P), (2 * P, 3 * P)):
+        early = tile([P, 2 * P], F32, "early")
+        late = tile([P, 2 * P], F32, "late")
+        for lo, hi, result in ((0, 2 * P, early[:]), (2 * P, 3 * P, late[:, :P])):
             acc = ring.tile([P, hi - lo], F32, name="acc")
             product(nc, acc[:], codes[:, :P], scales[:, :P], codes[:, P + lo : P + hi], scales[:, P + lo : P + hi])
-            nc.scalar.copy(out=early[:, lo:hi], in_=acc[:])
-        nc.sync.dma_start(out=out[:, 0 : (BLOCKS - 1) * P], in_=early[:])
+            nc.scalar.copy(out=result, in_=acc[:])
+        nc.sync.dma_start(out=out[:, 0 : 2 * P], in_=early[:])
 
         last_codes = tile([P, P], U32, "last_codes")
         last_scales = tile([P, P], U8, "last_scales")
         quantize(nc, last_codes[:], last_scales[:], last_grouped[:])
-        last_acc = ps.tile([P, P], F32, name="last_acc", tag="page_scores")
+        last_acc = ps.tile([P, P], F32, name="last_acc")
         product(nc, last_acc[:], codes[:, :P], scales[:, :P], last_codes[:], last_scales[:])
-        last = tile([P, P], F32, "last")
-        nc.vector.tensor_copy(out=last[:], in_=last_acc[:])
-        nc.sync.dma_start(out=out[:, (BLOCKS - 1) * P : E], in_=last[:])
+        nc.vector.tensor_copy(out=late[:, P:], in_=last_acc[:])
+        nc.sync.dma_start(out=out[:, 2 * P : E], in_=late[:])

from contextlib import ExitStack

import concourse.mybir as mybir
from concourse.masks import make_identity

D, T, I, Q, E, U = 512, 2048, 512, 128, 512, 512
FLOPS = 2 * D * Q * U + 2 * D * Q * I + 2 * I * Q * E

F32 = mybir.dt.float32
BF16 = mybir.dt.bfloat16
I32 = mybir.dt.int32
U32 = mybir.dt.uint32
U16 = mybir.dt.uint16
U8 = mybir.dt.uint8
FP8X4 = mybir.dt.float8_e4m3fn_x4
ALU = mybir.AluOpType
ACT = mybir.ActivationFunctionType

P = 128
PACK = 4
FLOOR = 0.05
BLOCKS = E // P


def interleave(copy, grouped, raw):
    copy(
        out=grouped.rearrange("p (c i) t -> p c t i", i=4),
        in_=raw.rearrange("p t (c i) -> p c t i", i=4),
    )


def quantize(nc, codes, scales, grouped):
    nc.vector.quantize_mx(out=codes.bitcast(FP8X4), scales=scales, in_=grouped.rearrange("p c t -> p (c t)"))


def product(nc, acc, lhs_codes, lhs_scales, rhs_codes, rhs_scales):
    nc.tensor.matmul_mx(
        out=acc,
        lhsT=lhs_codes.bitcast(FP8X4),
        lhsT_scale=lhs_scales,
        rhs=rhs_codes.bitcast(FP8X4),
        rhs_scale=rhs_scales,
        start=True,
        stop=True,
    )


def turn(nc, turned, grouped, rows, ident):
    words = rows.bitcast(F32)
    for u in range(2):
        nc.tensor.transpose(turned[:, u, :], words[:, u::2], ident)
    nc.scalar.copy(
        out=grouped.rearrange("p c t -> p (c t)").bitcast(F32).rearrange("p (c u) -> p c u", u=2),
        in_=turned.rearrange("p u c -> p c u"),
    )


def tile_attend_pagethreshold_kernel(
    tc, query, keys_words, keys_scales, pquery, pgsum, th, size, vals, offs, offs2, out
):
    nc = tc.nc
    with ExitStack() as ctx:
        lists = ctx.enter_context(tc.tile_pool(name="lists", bufs=1))
        sb = ctx.enter_context(tc.tile_pool(name="sb", bufs=1))
        ps = ctx.enter_context(tc.psum_pool(name="ps", bufs=1))
        ring = ctx.enter_context(tc.psum_pool(name="ring", bufs=2))

        def tile(shape, dtype, name, takes_over=None):
            return sb.tile(shape, dtype, name=name, tag=takes_over or name, align_bytes=64)

        token_list = lists.tile([P, I // 16], U16)
        page_list = lists.tile([P, I // 16], U16)
        pq_raw = tile([P, PACK, Q], F32, "pq_raw")
        pg_raw = tile([P, PACK, U], F32, "pg_raw")
        q_raw = tile([P, PACK, Q], F32, "q_raw")
        warm = tile([P, 1], F32, "warm")
        key_words = tile([P, T], U32, "key_words")
        key_bytes = tile([P, T], U8, "key_bytes")
        th_col = tile([P, 1], F32, "th_col")
        size_cols = tile([P, PACK], F32, "size_cols")
        val_pool = [tile([P, T], F32, "val_pool%d" % c) for c in range(BLOCKS)]

        nc.vector.memset(key_bytes[:].bitcast(I32), 0)
        nc.scalar.dma_start(out=th_col[:], in_=th)
        nc.gpsimd.memset(warm[:], 0.0)
        nc.scalar.activation(out=warm[:], in_=warm[:], func=ACT.Exp)
        nc.sync.dma_start(out=pq_raw[:], in_=pquery.rearrange("(p t) c -> p t c", t=PACK))
        nc.sync.dma_start(out=pg_raw[:], in_=pgsum.rearrange("(p t) c -> p t c", t=PACK))
        nc.sync.dma_start(token_list[:], offs)
        byte_rows = keys_scales[0].bitcast(I32).rearrange("(g r) n -> r g n", r=4)
        for r in range(4):
            nc.sync.dma_start(out=key_bytes[r:P:32, :].bitcast(I32), in_=byte_rows[r])
        nc.sync.dma_start(out=q_raw[:], in_=query.rearrange("(p t) c -> p t c", t=PACK))
        nc.sync.dma_start(
            out=key_words[:].bitcast(I32), in_=keys_words[0].rearrange("p n t -> p (n t)").bitcast(I32)
        )
        nc.sync.dma_start(page_list[:], offs2)
        for c in range(BLOCKS):
            if c == BLOCKS - 1:
                nc.sync.dma_start(out=size_cols[:], in_=size.rearrange("o (p t) -> (o p) t", t=PACK))
            nc.sync.dma_start(out=val_pool[c][:], in_=vals[c * P : (c + 1) * P, :])

        ident = tile([P, P], F32, "ident")
        make_identity(nc, ident[:])

        pq_grouped = tile([P, Q, PACK], BF16, "pq_grouped")
        pq_codes = tile([P, Q], U32, "pq_codes")
        pq_scales = tile([P, Q], U8, "pq_scales")
        interleave(nc.scalar.copy, pq_grouped[:], pq_raw[:])
        quantize(nc, pq_codes[:], pq_scales[:], pq_grouped[:])

        pg_codes = tile([P, U], U32, "pg_codes")
        pg_scales = tile([P, U], U8, "pg_scales")
        for h, copy in enumerate((nc.vector.tensor_copy, nc.scalar.copy)):
            cols = slice(h * U // 2, (h + 1) * U // 2)
            pg_grouped = tile([P, U // 2, PACK], BF16, "pg_grouped%d" % h)
            interleave(copy, pg_grouped[:], pg_raw[:, :, cols])
            quantize(nc, pg_codes[:, cols], pg_scales[:, cols], pg_grouped[:])
        page_scores = ps.tile([P, U], F32)
        product(nc, page_scores[:], pq_codes[:], pq_scales[:], pg_codes[:], pg_scales[:])

        k_scales = tile([P, I], U8, "k_scales")
        nc.vector.tensor_copy(out=k_scales[:], in_=key_bytes[:].indirect(token_list[:]))

        q_grouped = tile([P, Q, PACK], BF16, "q_grouped")
        q_codes = tile([P, Q], U32, "q_codes")
        q_scales = tile([P, Q], U8, "q_scales")
        interleave(nc.scalar.copy, q_grouped[:], q_raw[:])
        quantize(nc, q_codes[:], q_scales[:], q_grouped[:])

        shift = tile([P, 1], F32, "shift")
        nc.gpsimd.tensor_scalar(shift[:], th_col[:], -1.0, -FLOOR, ALU.mult, ALU.add)
        above = tile([P, U], F32, "above", takes_over="q_raw")
        nc.scalar.activation(out=above[:], in_=page_scores[:], func=ACT.Relu, bias=shift[:], scale=1.0)
        excess = tile([P, U], F32, "excess")
        nc.scalar.activation(out=excess[:], in_=above[:], func=ACT.Copy, bias=FLOOR, scale=1.0)

        k_codes = tile([P, I], U32, "k_codes")
        nc.vector.tensor_copy(out=k_codes[:], in_=key_words[:].indirect(token_list[:]))

        scores = ps.tile([P, I], F32)
        product(nc, scores[:], q_codes[:], q_scales[:], k_codes[:], k_scales[:])

        gate = tile([P, I], F32, "gate")
        for h in range(2):
            nc.vector.tensor_copy(
                out=gate[:, h * I // 2 : (h + 1) * I // 2],
                in_=excess[:].indirect(page_list[:, h * I // 32 : (h + 1) * I // 32]),
            )

        neg_max = tile([P, 1], F32, "neg_max")
        nc.vector.tensor_reduce(neg_max[:], scores[:], mybir.AxisListType.X, ALU.max, negate=True)
        expd = tile([P, I], F32, "expd")
        nc.scalar.activation(out=expd[:], in_=scores[:], func=ACT.Exp, bias=neg_max[:], scale=1.0)

        grouped = tile([P, BLOCKS * P, PACK], BF16, "grouped")
        last_grouped = tile([P, P, PACK], BF16, "last_grouped")

        def gather_values(c):
            listed = tile([P, I], BF16, "listed%d" % c)
            nc.vector.tensor_copy(out=listed[:], in_=val_pool[c][:].indirect(token_list[:]))
            turned = ring.tile([P, 2, P], F32, name="turned")
            target = last_grouped[:] if c == BLOCKS - 1 else grouped[:, (c + 1) * P : (c + 2) * P, :]
            turn(nc, turned[:], target, listed[:], ident[:])

        gather_values(0)

        weights = tile([P, I], F32, "weights", takes_over="val_pool0")
        row_sum = tile([P, 1], F32, "row_sum")
        nc.vector.scalar_tensor_tensor(weights[:], expd[:], 1.0, gate[:], ALU.mult, ALU.mult, accum_out=row_sum[:])
        inv_sum = tile([P, 1], F32, "inv_sum")
        nc.vector.reciprocal(inv_sum[:], row_sum[:])
        normed = tile([P, PACK, P], F32, "normed")
        nc.scalar.activation(
            out=normed[:].rearrange("q t s -> q s t"),
            in_=weights[:].rearrange("q (s t) -> q s t", t=PACK),
            func=ACT.Copy,
            scale=inv_sum[:],
        )
        w_turned = ps.tile([P, PACK, Q], F32)
        for t in range(PACK):
            nc.tensor.transpose(w_turned[:, t, :], normed[:, t, :], ident[:])

        gather_values(1)
        gather_values(2)
        nc.vector.tensor_tensor(
            grouped[:, :P, :],
            w_turned[:].rearrange("p t q -> p q t"),
            size_cols[:].unsqueeze(1).to_broadcast([P, Q, PACK]),
            ALU.mult,
        )
        gather_values(3)

        codes = tile([P, BLOCKS * P], U32, "codes", takes_over="val_pool3")
        scales = tile([P, BLOCKS * P], U8, "scales")
        quantize(nc, codes[:], scales[:], grouped[:])
        early = tile([P, 2 * P], F32, "early")
        late = tile([P, 2 * P], F32, "late")
        for lo, hi, result in ((0, 2 * P, early[:]), (2 * P, 3 * P, late[:, :P])):
            acc = ring.tile([P, hi - lo], F32, name="acc")
            product(nc, acc[:], codes[:, :P], scales[:, :P], codes[:, P + lo : P + hi], scales[:, P + lo : P + hi])
            nc.scalar.copy(out=result, in_=acc[:])
        nc.sync.dma_start(out=out[:, 0 : 2 * P], in_=early[:])

        last_codes = tile([P, P], U32, "last_codes")
        last_scales = tile([P, P], U8, "last_scales")
        quantize(nc, last_codes[:], last_scales[:], last_grouped[:])
        last_acc = ps.tile([P, P], F32, name="last_acc")
        product(nc, last_acc[:], codes[:, :P], scales[:, :P], last_codes[:], last_scales[:])
        nc.vector.tensor_copy(out=late[:, P:], in_=last_acc[:])
        nc.sync.dma_start(out=out[:, 2 * P : E], in_=late[:])
